import numpy as np, ml_dtypes
CORES = [66,74,82,90,194,202,210,218]
N = 8
BF = ml_dtypes.bfloat16
def gentries(a):
    return np.ascontiguousarray(a.reshape(8, 16, -1).transpose(0, 2, 1)).reshape(8, -1)
def gtable(e):
    e = np.asarray(e); return np.ascontiguousarray(e.reshape(8, -1, 16).transpose(0, 2, 1)).reshape(128, -1).astype(np.int32)
P, L, J, RO, NEED = 512, 4096, 16, 3, 8
def parts(rng):
    share = rng.choice(np.array([0.03, 0.06, 0.12, 0.25, 0.4]), (N, 8, 1, 1))
    dic = np.where(rng.random((N, 8, 1, L)) < share, rng.integers(0, 6, (N, 8, 16, L), dtype=np.int8), rng.integers(6, 16, (N, 8, 16, L), dtype=np.int8))
    pup = (rng.random((N, 8, 16, P)) * rng.integers(2, 13, (N, 8, 1, P))).astype(np.int8)
    return dic, pup, np.argsort(rng.random((N, 8, P)), axis=-1), rng.integers(0, 4096, (N, 8, 16, 1))
def pack(dic, pup, seat, wt):
    return {"dic": dic.astype(np.float32).reshape(N, 128, L).astype(BF), "pup": pup.astype(np.float32).reshape(N, 128, P).astype(BF),
            "seat": np.stack([gtable(a) for a in seat]), "wt": np.ascontiguousarray(wt.reshape(N, 128, 1)).astype(np.int32)}
def setup_inputs(rng):
    return pack(*parts(rng))
def setup_inputs_spread(rng):
    hard = rng.choice(np.array([0.6, 0.85, 0.97]), (N, 8, 1, 1))
    a = np.where(rng.random((N, 8, 1, L)) < hard, 0.1, rng.choice(np.array([0.5, 1.0, 2.0, 6.0]), (N, 8, 1, L)))
    dic = np.minimum(16 * rng.random((N, 8, 16, L)) ** a, 15).astype(np.int8)
    pup = np.minimum(16 * rng.random((N, 8, 16, P)) ** rng.choice(np.array([0.3, 1.0, 2.0, 4.0, 8.0]), (N, 8, 1, P)), 15).astype(np.int8)
    wt = np.minimum(np.exp2(12 * rng.random((N, 8, 16, 1))) - 1, 4095).astype(np.int64)
    return pack(dic, pup, np.argsort(rng.random((N, 8, P)), axis=-1), wt)
def setup_inputs_ends(rng):
    kind = (7 - np.arange(8)[None, :] + N - 1 - np.arange(N)[:, None]) % 4; k4 = kind[:, :, None, None]
    hard = np.where(rng.random((N, 8, 1, L)) < np.where(k4 == 0, 0.6, 0.96), 0.95, 0.3)
    dic = 15 * (rng.random((N, 8, 16, L)) < hard)
    pup = 15 * (rng.random((N, 8, 16, P)) >= rng.choice(np.array([0.6, 0.9, 0.97, 1.0]), (N, 8, 1, P)))
    wt = 4095 * ((rng.random((N, 8, 16, 1)) < 0.6) | (k4 == 0)); wt[:, :, 0] = 4095; wt[:, :, 15] = np.where(kind == 0, 4095, 0)[:, :, None]
    shut = (k4 == 1) & (np.arange(16)[:, None] >= NEED - 1)
    dic = np.where(shut, 15, dic); pup = np.where(shut, 0, pup)
    half = np.arange(P // 2); z = np.stack([half, P - 1 - half], 1).reshape(-1)
    seat = np.stack([np.stack([np.roll(z[::int(rng.choice(np.array([-1, 1])))], int(rng.integers(0, P))) for g in range(8)]) for r in range(N)])
    for r in range(N):
        for g in range(8):
            a = seat[r, g]; one = a[np.array([0, 2, 5, P - J, P - 1])]
            pup[r, g][:, one] = 0; pup[r, g][0, one] = 1
            if kind[r, g] != 1: pup[r, g][:, a[np.array([4, P - 2])]] = 15
    return pack(dic, pup, seat, wt)
def setup_inputs_corners(rng):
    dic, pup, seat, wt = parts(rng); c = int(rng.integers(0, 8))
    for r in range(N):
        for g in range(8):
            k = (r + g + c) % 8
            if k == 0: dic[r, g] = 0
            if k == 1: pup[r, g] = 0; dic[r, g] = np.maximum(dic[r, g], 1)
            if k == 2: wt[r, g] = 0; dic[r, g][:, 111] = 0
            if k == 3: wt[r, g] = 4095
            if k == 4:
                m = np.where(rng.random(L) < 0.1, NEED, NEED - 1); low = np.argsort(rng.random((16, L)), axis=0) < m
                dic[r, g] = np.where(low, rng.integers(0, 8, (16, L)), 15); pup[r, g] = rng.integers(7, 15, (16, P))
            if k == 5: dic[r, g] = 15 - (rng.random((16, L)) < 0.1); pup[r, g] = 15 - np.where(rng.random((16, P)) < 0.35, 0, rng.integers(1, 4, (16, P)))
            if k == 6: dic[r, g] = 7 + (rng.random((16, L)) < 0.6); pup[r, g] = 7 + (rng.random((16, P)) < 0.2)
            if k == 7:
                dic[r, g] = 8; pup[r, g] = rng.integers(0, 3, (16, P)); e = seat[r, g][J - 1::J]
                pup[r, g][:, e] = rng.integers(8, 16, (16, P // J))
    return pack(dic, pup, seat, wt)
def wn(a, b, j=0, t=0):
    return ((a * b >> 5) + 37 * j + 11 * t) & (L - 1)
def hexed(rng, three, kk, lo, hi):
    x = rng.integers(lo, hi + 1, (16, P)); x[three] = (kk[None, :] >> np.array([[0], [4], [8]])) & 15
    return x
def rule(rng, three, hard):
    d = np.where(hard, 15, rng.integers(0, 6, (16, L))); d[three] = rng.integers(0, 16, (3, L))
    return d
def setup_inputs_full(rng):
    dic, pup, seat, wt = parts(rng); c = int(rng.integers(0, 8)); S = P // J
    K = np.arange(4096); V = (K * K >> 5) & (P - 1); W0 = wn(K, K); top = int(V[4095]); z = P - J + 1; every = np.arange(L)
    for g in range(8):
        k = (g + c) % 8; three = rng.permutation(16)[:3]; rest = np.setdiff1d(np.arange(16), three)
        if k < 5: wt[:, g] = 0; wt[:, g, three, 0] = np.array([1, 16, 256])
        if k < 4:
            h1 = wn(4095, 4094)
            sp = int(rng.choice(np.flatnonzero((z - V >= 0) & (z - V < J) & (W0 != h1) & (W0 != wn(4094, 4094))))); jz = z - int(V[sp])
            hs = np.array([h1, int(W0[sp])]); own = K[~np.isin(W0, hs)]; line = {}
            for r in range(N):
                if r % 2 == k % 2: continue
                kk = rng.choice(own, P); kk[top] = 4094; kk[P - 1] = sp
                kk[top + 1] = rng.choice(own[~np.isin(wn(4095, own, 1), hs)]); kk[0] = rng.choice(own[~np.isin(wn(181, own, 1), hs)])
                line[r] = kk; pup[r, g][:, seat[r, g]] = hexed(rng, three, kk, 6, 14); dic[r, g] = rule(rng, three, np.isin(every, hs))
            for r in range(N):
                if r % 2 != k % 2: continue
                kb = line[(r + 1) % N]
                s = K[~np.isin(V, np.array([0, P - 1, top, top + 1])) & ~np.isin(wn(K, kb[V]), hs) & (wn(sp, K, jz) != W0)]
                s = rng.permutation(s); s = rng.permutation(s[np.unique(V[s], return_index=True)[1]])
                more = [4095]
                if k >= 2: more = more + [181, int(rng.choice(np.flatnonzero((V == 0) & ~np.isin(wn(K, kb[0]), hs))))]
                kk = rng.integers(0, 4096, P); kk[0] = 4095
                kk[1::J] = np.concatenate([rng.permutation(np.concatenate([np.array(more), s[:S - 1 - len(more)]])), s[-1:]])
                x = hexed(rng, three, kk, 0, 13); x[:, 0] = 15; x[rest, z] = 14
                d = rule(rng, three, every >= 0); d[rest, wn(sp, int(kk[z]), jz)] = 14
                pup[r, g][:, seat[r, g]] = x; dic[r, g] = d
        if k == 4:
            sa = int(rng.choice(np.flatnonzero(V == P - 1))); ha = int(wn(sa, sa, 0, 1))
            sb = int(rng.choice(np.flatnonzero((K >= 64) & (V < P - J) & (W0 != W0[sa])))); hb = int(W0[sb]); u = int(V[sb])
            own = K[~np.isin(W0, np.array([ha, hb, ha - 11, hb - 11]) & (L - 1))]
            au = own[~np.isin(wn(sb, own), np.array([ha, hb])) & (wn(sa, own, 0, 1) != hb)]
            for r in range(N):
                kk = rng.choice(own, P); kk[u] = rng.choice(au); kk[P - 1] = sa if r < 2 else sb
                pup[r, g][:, seat[r, g]] = hexed(rng, three, kk, 6, 14); dic[r, g] = rule(rng, three, every == (ha if r < 2 else hb))
        if k == 5:
            for r in range(N):
                dic[r, g] = rng.integers(6, 12, (16, L))
                pup[r, g][:, seat[r, g]] = np.where((np.arange(P) + r) % 2 == 0, rng.integers(0, 6, (16, P)), rng.integers(12, 15, (16, P)))
        if k >= 6:
            wt[:, g] = rng.integers(4090, 4096, (N, 16, 1)) if k == 6 else 4095
            for r in range(N):
                x = 13 + (rng.random((16, P)) < 0.7) + (rng.random((16, P)) < 0.15)
                x = np.minimum(x, 15); x[:, np.array([P // 2, P - 1])] = 15
                pup[r, g][:, seat[r, g]] = x
                dic[r, g] = np.where(rng.random(L) < (0.7 if k == 6 else 0.9), 15, rng.integers(0, 14, (16, L)))
    return pack(dic, pup, seat, wt)
def check_inputs(d):
    bad = []
    for k, lo, hi in (("dic", 0, 15), ("pup", 0, 15), ("seat", 0, P - 1), ("wt", 0, 4095)):
        a = np.asarray(d[k]).astype(np.float64)
        if not (np.all(a >= lo) and np.all(a <= hi)): bad.append("range of " + k)
        elif not np.all(a == np.floor(a)): bad.append("whole numbers of " + k)
    for a in d["seat"]:
        if not np.all(np.sort(gentries(np.asarray(a)), axis=1) == np.arange(P)):
            bad.append("permutation of seat"); break
    return bad
def keys(x, o, w):
    xo = np.take_along_axis(x, o[:, None, :], 2)
    return xo, np.add.reduce(xo.astype(np.int64) * w, axis=1) & 4095
def reference(dic, pup, seat, wt):
    d = dic.astype(np.float32).astype(np.int16).reshape(N, 8, 16, L); x = pup.astype(np.float32).astype(np.int16).reshape(N, 8, 16, P)
    o = np.stack([gentries(a) for a in seat]).astype(np.int64); w = wt.astype(np.int64).reshape(N, 8, 16, 1)
    q = np.arange(P); jj = np.arange(J); pl = q[:, None] + jj; inside = pl < P; pc = np.minimum(pl, P - 1)
    for t in range(RO):
        away = []
        for r in range(N):
            xo, s = keys(x[r], o[r], w[r])
            ix = (((s[:, :, None] * s[:, pc]) >> 5) + 37 * jj + 11 * t) & (L - 1)
            D = np.take_along_axis(d[r], ix.reshape(8, 1, -1), 2)
            ok = inside & (np.add.reduce((xo[:, :, pc] >= D.reshape(8, 16, P, J)).astype(np.int16), axis=1) >= NEED)
            found = np.any(ok, axis=2); last = np.where(found, q + np.argmax(ok, axis=2), np.minimum(q + J - 1, P - 1))
            st = np.zeros((8, P), np.int64)
            for g in range(8):
                f = last[g].tolist(); p = 0
                while p < P:
                    st[g, p:f[p] + 1] = p; p = f[p] + 1
            fs = np.take_along_axis(found, st, 1); ls = np.take_along_axis(last, st, 1)
            D2 = np.take_along_axis(D, (st * J + q - st)[:, None, :], 2)
            xo = xo + ((fs & (q < ls))[:, None, :] & (D2 > xo))
            x[r] = np.take_along_axis(xo, np.argsort(o[r], axis=1)[:, None, :], 2)
            o[r] = np.take_along_axis(o[r], np.where(fs, np.where(q == st, ls, q - 1), q), 1)
            away.append((q == st) & ~fs)
        now = [keys(x[r], o[r], w[r]) for r in range(N)]; x0 = x.copy()
        for a in range(N):
            b = (a + 1 + t % (N - 1)) % N; xb, sb = now[b]
            for g in range(8):
                ps = np.flatnonzero(away[a][g])
                if len(ps) == 0: continue
                sv = now[a][1][g, ps]
                v = ((((sv * sv) >> 5) & (P - 1))[:, None] + jj) & (P - 1)
                D = d[b, g][:, (((sv[:, None] * sb[g, v]) >> 5) + 37 * jj + 11 * t) & (L - 1)]
                ok = (np.add.reduce((xb[g][:, v] >= D).astype(np.int16), axis=0) >= NEED) & ~away[b][g, v]
                h = np.flatnonzero(np.any(ok, axis=1))
                if len(h) == 0: continue
                u, i = np.unique(v[h, np.argmax(ok[h], axis=1)], return_index=True)
                pa = o[a][g, ps[h[i]]]; pb = o[b][g, u]
                x[a, g][:, pa] = x0[b, g][:, pb]; x[b, g][:, pb] = x0[a, g][:, pa]
    return {"ypup": x.reshape(N, 128, P).astype(np.float32).astype(BF), "yseat": o.astype(np.float32)}

import math
from concourse.mybir import AluOpType as ALU, AxisListType as AX, ActivationFunctionType as AF

BF, F32, F16, I32, U16 = "bfloat16", "float32", "float16", "int32", "uint16"
SJ = [15, 14, 13, 12, 11, 10, 9]
RO = 3
SB = {
    "D": (4688, BF), "PU": (512, BF), "SE": (32, I32), "WT": (4, I32), "SU": (32, U16),
    "X0": (1072, BF), "X1": (1072, BF), "O0": (512, F32), "O1": (1040, F32), "Y": (1040, BF),
    "CMP": (9216, BF), "DG": (1536, BF), "KR": (1040, F32), "IB": (128, BF), "UR": (80, F32),
    "KI": (32, I32), "KA": (128, I32), "K16": (40, F16), "PR": (512, I32), "IX": (512, U16),
    "RP": (512, BF), "LN1": (32, F32), "J1": (32, I32), "OFF": (32, U16),
    "LN2": (64, F32), "J2": (64, I32), "SG": (64, BF), "NS": (64, BF), "JJ": (64, BF),
    "T1": (1536, BF), "U2": (32, U16), "T2": (640, F32), "CH": (128, U16), "UU": (80, BF),
    "W1": (72, BF), "W2": (64, BF), "AW": (64, BF),
    "RL": (32, F32), "LN3": (32, F32), "J3": (32, I32), "LF": (32, F32), "LU": (32, U16),
    "MV": (32, F32), "SRI": (32, I32), "SRU": (32, U16), "SOI": (32, I32), "SOU": (32, U16),
    "VD": (32, F32), "VL": (4, F32), "VU": (8, U16), "INC": (512, BF),
    "PK": (288, F32), "LA": (288, F32), "RT": (96, BF), "LB": (96, BF),
    "PLU": (32, U16), "PLD": (32, F16), "VXH": (32, BF), "INV": (32, BF),
    "XG": (512, BF), "K2": (32, I32), "IX2": (32, U16), "CM2": (512, BF), "EP": (32, BF), "F1": (32, F32),
    "FP": (32, F16), "CD": (32, F32), "CL": (4, F32), "EQ": (64, F32), "LO": (4, F32), "FI": (8, U16),
    "OLU": (32, U16), "VP": (32, F32), "VQ": (4, F32), "VPU": (8, U16),
    "PI": (4, I32), "COL": (40, F32), "IR": (128, F32), "GA": (128, F32), "ZI": (144, F32), "ZM": (144, F32),
    "ROT": (31 * 128, BF), "IDB": (128, BF), "NIB": (128, BF), "C2K": (128, F16),
    "ZW": (144, F16), "Z1": (144, BF), "ZH": (144, BF), "Z16": (144, BF), "Z8": (144, BF), "Z8F": (144, F32),
    "BLK": (128, F32), "BL16": (128, BF), "BW": (128, F16), "BP": (256, F16), "BS": (512, BF), "TP": (768, BF),
    "TRI": (128, BF), "TR0": (128, BF), "M32": (32, F32), "I16": (16, F32), "B128": (16, F32), "DM": (32, F32),
    "SC": (64, F32), "PW": (32, F32), "CT0": (512, F32), "CT": (512, F32), "T2C": (128, F32),
    "Q16": (32, F16), "QF": (32, F32), "QB": (32, F32), "VC": (32, F16), "DUM": (32, F32), "CC3": (96, F16), "CCT": (64, F32),
}
PS = ["E0", "E1", "CA", "CB", "KB0", "KB1", "PA", "PB"]
SB.update({"SEL": (2048, BF), "PLT": (1040, F32), "V0I": (32, I32), "V16": (32, F16), "NS1": (64, BF), "AWN": (32, F32),
           "KP": (32, F32), "C64": (32, BF), "KT": (32, F32), "SOT": (32, F32), "NBL": (128, BF), "PLI": (32, I32)})
WHERE = {}
SCRATCH = {}
for _k, (_w, _d) in SB.items():
    if _w <= 144 and _k not in ("SE", "WT", "RT", "LB"):
        _n = "pool_" + _d; _o = SCRATCH[_n][1][1] if _n in SCRATCH else 0
        WHERE[_k] = (_n, _o); SCRATCH[_n] = ("sbuf", [128, _o + (_w + 15) // 16 * 16], _d)
    else:
        WHERE[_k] = (_k, 0); SCRATCH[_k] = ("sbuf", [128, _w], _d)
for _p in PS:
    SCRATCH[_p] = ("psum", [128, 512], F32)
SEMAPHORES = ["sv", "ss", "sp", "sg", "sent", "dse", "dpu", "dwt", "ddi", "dde", "dy", "dz", "f0", "f1", "f2", "f3"] + \
    ["a%d" % t for t in range(RO)] + ["b%d" % t for t in range(RO)]
ESEM = {"V": "sv", "S": "ss", "P": "sp", "G": "sg"}
C16, C16X8, WF, WH, P4, N4, NN4, P16, THR, THV, THS, J32, HI, LO512, PAR, BP0, BP1 = range(17)
RC, PC, S4, CJ, DUMC = 17, 21, 25, 29, 32
CYC, LAT = 1.04, 60.0
LOOKS, PASSES = [0.15, 0.3, 0.6], 4
EARLY, FIRST = 30000.0, ("PI", "COL", "GA", "M32", "DM", "BLK", "SC", "PW", "I16", "BS", "BL16")
CHUNKS = [(0, 2), (2, 4), (4, 8), (8, 12), (12, 16)]
NG = 7


def build(T, topo, core, rank):
    ops = []; late = [False]

    def a(name, lo=0, hi=None, st=1):
        return ("a", name, lo, (SB[name][0] if name in SB else 512) if hi is None else hi, st)

    def c(k):
        return a("COL", k, k + 1)

    def ind(win, off):
        return ("i", win, off)

    def isop(x):
        return isinstance(x, tuple)

    def ap(x):
        if not isop(x):
            return x
        if x[0] == "i":
            return ap(x[1]).indirect(ap(x[2]))
        nm, o = WHERE.get(x[1], (x[1], 0))
        return T[nm][:, o + x[2]:o + x[3]] if x[4] == 1 else T[nm][:, o + x[2]:o + x[3]:x[4]]

    def n_of(x):
        return 16 * n_of(x[2]) if x[0] == "i" else len(range(x[2], x[3], x[4]))

    def spans(xs):
        r = []
        for x in xs:
            if isop(x):
                r += [x[1][1:], x[2][1:]] if x[0] == "i" else [x[1:]]
        return r

    def add(eng, fn, outs, ins, cost, **kw):
        rd = spans(ins); wr = []
        for o in outs:
            if o[0] == "i":
                wr.append(o[1][1:]); rd.append(o[2][1:])
            else:
                wr.append(o[1:])
        up = EARLY if not late[0] and wr and wr[0][0] in FIRST else 0.0
        ops.append(dict(eng=eng, fn=fn, rd=rd, wr=wr, cost=cost, up=up, **kw))

    def vcost(out, x, per=1.0):
        n = n_of(out)
        if out[0] == "i":
            return 55 + 3.5 * n * CYC
        if isop(x) and x[0] == "i":
            return 55 + 1.56 * n * CYC
        if isop(x) and x[1] in SB and out[1] in SB and SB[x[1]][1] in (BF, F16, U16) and SB[out[1]][1] in (BF, F16, U16) and per == 1.0:
            per = 0.5
        return max(64, per * n) * CYC

    def cp(out, x):
        add("V", lambda q: q.tensor_copy(ap(out), ap(x)), [out], [x], vcost(out, x))

    def tt(out, x, y, op):
        per = 1.0 if (x[1] in PS or y[1] in PS) else 2.0
        add("V", lambda q: q.tensor_tensor(ap(out), ap(x), ap(y), op), [out], [x, y], vcost(out, x, per))

    def ts(out, x, s1, op0, s2=None, op1=None):
        if op1 is None:
            add("V", lambda q: q.tensor_scalar(ap(out), ap(x), ap(s1), None, op0), [out], [x, s1], vcost(out, x))
        else:
            add("V", lambda q: q.tensor_scalar(ap(out), ap(x), ap(s1), ap(s2), op0, op1), [out], [x, s1, s2], vcost(out, x))

    def red(out, x, op):
        add("V", lambda q: q.tensor_reduce(ap(out), ap(x), AX.X, op), [out], [x], max(64, n_of(x)) * CYC)

    def scan(out, d0, d1, init, op0, op1):
        add("V", lambda q: q.tensor_tensor_scan(ap(out), ap(d0), ap(d1), init, op0, op1), [out], [d0, d1], 64 * CYC)

    def ms(out, v):
        add("V", lambda q: q.memset(ap(out), v), [out], [], vcost(out, out))

    def act(out, x, f, bias=0.0, scale=1.0):
        cost = 70 + 1.56 * n_of(out) * CYC if x[0] == "i" else max(64, n_of(out)) * CYC
        add("S", lambda q: q.activation(ap(out), ap(x), f, bias=ap(bias), scale=ap(scale)), [out], [x, bias, scale], cost)

    gid = [0]

    def mms(items, wide=1):
        gid[0] += 1
        lead = any(o != items[0][0] for o, l, r in items)
        for o, l, r in items:
            mm(gid[0], o, l, r, wide, lead)

    def mm(grp, o, l, r, wide=1, lead=False):
        add("P", lambda q, st, sp: q.matmul(ap(o), ap(l), ap(r), st, sp), [o], [l, r], max(64, n_of(r)) * 0.52 * wide, grp=grp, lead=lead)

    def iota(out, pat, base, cm):
        cost = 130 + 2 * n_of(out) * CYC
        if SB[out[1]][1] == I32:
            add("G", lambda q: q.iota(ap(out), pat, base, cm), [out], [], cost)
        else:
            add("G", lambda q: q.iota(ap(out), pat, base, cm, allow_small_or_imprecise_dtypes=True), [out], [], cost)

    def asel(out, x, op, fill, base, sign):
        add("G", lambda q: q.affine_select(ap(out), ap(x), [[-sign, 128]], op, fill, base, sign), [out], [x], 170 + 256 * CYC)

    def dma(eng, fn, outs, ins, sem, lat):
        add(eng, fn, outs, ins, 60, dsem=sem, dn=16, lat=lat)

    def send(src, land, sem, to):
        dst = T.cores[to]
        rid, pid = topo.addr(dst, core); m = topo.mask(core, dst); k = len(topo.engines(core, dst))
        add("G", lambda q: q.remote_dma(ap(land), ap(src), T.sem[sem], T.sem["sent"], pid, rid, m), [], [src], 300, remote=k)
        return len(ops) - 1

    def recv(land, sem, frm, after):
        k = len(topo.engines(T.cores[frm], core))
        add("R", None, [land], [], 0, dsem=sem, dn=k, lat=2500, after=after)

    def Z(name, r):
        return a(name, 15 - r, 143 - r)

    def ROT(d):
        return a("ROT", (d + 15) * 128, (d + 16) * 128)

    M, A_, SUB = ALU.mult, ALU.add, ALU.subtract
    VJ = [j for j in range(16) if j not in SJ]
    order = SJ[:2] + VJ[:2] + SJ[2:4] + VJ[2:4] + SJ[4:] + VJ[4:]
    dma("Y", lambda q: q.dma_start(T.SE[:, 0:32], T.seat[:]), [a("SE")], [], "dse", 2000)
    dma("S", lambda q: q.dma_start(T.WT[:, 0:1], T.wt[:]), [a("WT")], [], "dwt", 2000)
    dma("Y", lambda q: q.dma_start(T.PU[:, 0:512], T.pup[:]), [a("PU")], [], "dpu", 2200)
    dma("S", lambda q: q.dma_start(T.D[:, 0:4096], T.dic[:]), [a("D", 0, 4096)], [], "ddi", 5000)
    dma("Y", lambda q: q.dma_start(T.D[:, 4096:4688], T.dic[:, 0:592]), [a("D", 4096, 4688)], [], "dde", 5000)
    ops[2]["then"] = 0; ops[3]["then"] = 1; ops[4]["then"] = 2
    iota(a("PI", 0, 1), [[0, 1]], 0, 1)
    iota(a("ZI"), [[1, 144]], -15, -1)
    iota(a("IR"), [[112, 8], [-1, 16]], 0, -7)
    iota(a("M32"), [[0, 2], [1, 16]], 0, 0)
    iota(a("O1", 0, 512), [[1, 512]], 0, 0)
    iota(a("O1", 512, 1040), [[1, 528]], 512, 0)
    iota(a("KR", 512, 1040), [[0, 528]], 0, 0); iota(a("Y", 512, 1040), [[0, 528]], 0, 0)
    iota(a("X0", 528, 1072), [[0, 544]], -64, 0)

    def fill(out, x, sem):
        dma("Y", lambda q: q.dma_start(ap(out), ap(x)), [out], [x], sem, 2200)
    fill(a("PLT", 512, 1040), a("KR", 512, 1040), "f0")
    fill(a("CMP", 8208, 8720), a("Y", 512, 1024), "f1"); fill(a("CMP", 8720, 9216), a("Y", 512, 1008), "f2")
    fill(a("X1", 528, 1072), a("X0", 528, 1072), "f3")
    iota(a("GA"), [[16, 8], [0, 16]], 0, -1)
    ts(a("PI", 1, 2), a("PI", 0, 1), 15, ALU.bitwise_and)
    ts(a("PI", 2, 3), a("PI", 0, 1), 1, ALU.bitwise_and)
    cp(c(C16), a("PI", 1, 2)); cp(c(PAR), a("PI", 2, 3))
    ts(c(C16X8), c(C16), 8.0, M); ts(c(J32), c(C16), 32.0, M)
    ts(a("ZM"), a("ZI"), c(C16), A_, 0.0, ALU.is_equal)
    ts(c(WH), a("WT", 0, 1), 2048.0, ALU.is_gt, -4096.0, M)
    tt(c(WF), c(WH), a("WT", 0, 1), A_)
    ts(a("ZW"), a("ZM"), c(WF), M)
    cp(a("SU"), a("SE"))
    cp(a("X0", 0, 256), ind(a("PU"), a("SU", 0, 16)))
    act(a("X0", 256, 512), ind(a("PU"), a("SU", 16, 32)), AF.Identity)
    ms(a("X0", 512, 528), -64.0); ms(a("C64"), 64.0)
    ms(a("C2K"), 2048.0); ms(a("K16", 32, 40), 0.0)
    ts(a("IB"), a("IR"), c(C16X8), A_)
    ts(a("BLK"), a("GA"), c(C16), A_, 0.0, ALU.is_equal)
    act(a("BL16"), a("BLK"), AF.Identity)
    ong = [d for j in order[16 - NG:] if j for d in (j, j - 16)]
    for d in range(-15, 16):
        if d in ong:
            asel(ROT(d), a("BL16"), ALU.is_equal, 0.0, -d, 1)
        else:
            ts(ROT(d), a("IB"), float(d), ALU.is_equal)
    act(a("Z1"), a("ZM"), AF.Identity); act(a("ZH"), a("ZM"), AF.Identity, scale=0.5)
    ts(a("IDB"), a("IB"), 0.0, ALU.is_equal)
    act(a("NIB"), a("IDB"), AF.Identity, scale=-1.0)
    ts(a("DM"), a("M32"), c(C16), ALU.is_equal)
    act(a("I16"), a("DM", 0, 16), AF.Identity); act(a("B128"), a("DM", 0, 16), AF.Identity, scale=128.0)
    ms(a("SC", 0, 16), 4.0); ms(a("SC", 16, 32), 0.25); ms(a("SC", 32, 48), 0.0); ms(a("SC", 48, 49), 16.0 ** -7.5)
    scan(a("PW", 0, 16), a("SC", 0, 16), a("SC", 32, 48), 0.25, M, A_)
    scan(a("PW", 16, 32), a("SC", 16, 32), a("SC", 32, 48), 4.0, M, A_)
    tt(a("PW"), a("PW"), a("DM"), M)
    red(c(P4), a("PW", 0, 16), A_); red(c(N4), a("PW", 16, 32), A_)
    act(c(NN4), c(N4), AF.Identity, scale=-1.0)
    ts(c(P16), c(N4), c(N4), M, 2.0 ** 32, M)
    act(c(THR), a("SC", 48, 49), AF.Ln)
    lo = min(SJ)
    ts(c(THV), c(C16), float(lo), ALU.is_lt, 8.0, M)
    act(c(THS), c(THV), AF.Identity, bias=1.0)
    ts(c(HI), c(C16), 8.0, ALU.is_ge); ts(c(LO512), c(C16), 8.0, ALU.is_lt, 512.0, M)
    act(c(BP0), c(C16), AF.Identity, bias=-528.0); act(c(BP1), c(C16), AF.Identity, bias=-520.0)
    for k in range(16):
        act(a("SEL", 128 * k, 128 * k + 128), a("BLK"), AF.Identity, scale=a("I16", k, k + 1))
    for h in range(4):
        act(c(RC + h), c(C16), AF.Identity, bias=16.0 * h); act(c(PC + h), c(PAR), AF.Identity, bias=16.0 * h)
        act(c(S4 + h), c(P4), AF.Identity, scale=4.0 ** (8 * h - 16))
        act(a("BS", 128 * h, 128 * h + 128), a("BLK"), AF.Identity, scale=c(S4 + h))
    for t in range(RO):
        act(c(CJ + t), c(C16), AF.Identity, bias=11.0 * t, scale=37.0)
    for h in range(2):
        act(c(DUMC + h), c(C16), AF.Identity, bias=1040.0 + 16 * h)
    act(a("Z16"), a("ZM"), AF.Identity, scale=c(P16))
    act(a("Z8"), a("ZM"), AF.Identity, scale=a("I16", 8, 9)); act(a("Z8F"), a("ZM"), AF.Identity, scale=a("I16", 8, 9))
    ts(a("BW"), a("BLK"), c(WF), M)
    ts(a("BP", 0, 128), a("BLK"), c(BP0), M); ts(a("BP", 128, 256), a("BLK"), c(BP1), M)
    iota(a("T1", 512, 1536), [[64, 2], [2, 8], [0, 64]], 0, 0)
    for par in range(2):
        iota(a("CT0", par, 512, 2), [[1, 8], [16, 4], [64, 8]], 8 * par - 512, 0)
        iota(a("T2C", par, 128, 2), [[2, 64]], par + (15 if par else 1), 0)
    for k in range(8):
        act(a("CT", 64 * k, 64 * k + 64), a("CT0", 64 * k, 64 * k + 64), AF.Identity, scale=a("I16", k, k + 1))
    act(a("T2", 512, 640), a("T2C"), AF.Identity, scale=c(HI), bias=c(LO512))
    GE = ALU.is_ge
    asel(a("TP", 0, 128), a("BS", 0, 128), GE, 0.0, -1, 1)
    asel(a("TP", 128, 256), a("BS", 128, 256), GE, 0.0, 7, 1)
    asel(a("TP", 256, 384), a("BS", 256, 384), GE, 0.0, -1, -1)
    asel(a("TP", 384, 512), a("BS", 384, 512), GE, 0.0, -9, -1)
    asel(a("TP", 512, 640), a("BS", 256, 384), ALU.is_equal, 0.0, 0, 1)
    asel(a("TP", 640, 768), a("BS", 384, 512), ALU.is_equal, 0.0, 8, 1)
    act(a("TRI"), a("BLK"), AF.Identity, scale=-2048.0); act(a("NBL"), a("BLK"), AF.Identity, scale=-1.0)
    asel(a("TR0"), a("TRI"), GE, 0.0, -1, -1)
    asel(a("TRI"), a("TR0"), ALU.not_equal, 2048.0, 0, 1)
    iota(a("F1"), [[1, 32]], 1040 - 2048, 0)
    iota(a("QF"), [[16, 32]], 0, 0)
    ts(a("Q16"), a("QF"), c(C16), A_); ts(a("VC"), a("QF"), 528.0, A_)
    ts(a("QB"), a("Q16"), -512.0, A_, 1.0 / 512, M)
    iota(a("DUM"), [[1, 32]], 1040, 0)
    iota(a("CCT"), [[-16, 2], [1, 32]], 0, 0)
    ts(a("CCT"), a("CCT"), c(C16), GE, -2048.0, M)
    cp(a("CC3", 0, 32), a("DUM"))
    for h in range(2):
        tt(a("CC3", 32 + 32 * h, 64 + 32 * h), a("CCT", 32 * h, 32 * h + 32), a("DUM"), A_)
    ms(a("W1", 0, 2), 0.0); ms(a("CMP", 0, 7696, 513), 0.0);
    act(a("O0"), ind(a("O1", 0, 512), a("SU")), AF.Identity)

    late[0] = True
    L16, L4 = math.log(16.0), math.log(4.0)
    SHR, AND = ALU.arith_shift_right, ALU.bitwise_and

    def keys(bank, x):
        mms([(a(bank, 0, 32), Z("ZW", r), a(x, r, 512, 16)) for r in range(16)])

    def diag(row, tmp, cols):
        tt(a(tmp), row, a("DM"), M)
        for h in range(2):
            red(a(cols, h, h + 1), a(tmp, 16 * h, 16 * h + 16), A_)

    for t in range(RO):
        X, XN = "X%d" % (t % 2), "X%d" % ((t + 1) % 2)
        O, ON = "O%d" % (t % 2), "O%d" % ((t + 1) % 2)
        pk0, pk1, pk2 = [a("PK", 96 * t + 32 * k, 96 * t + 32 * k + 32) for k in range(3)]
        la0, la1, la2 = [a("LA", 96 * t + 32 * k, 96 * t + 32 * k + 32) for k in range(3)]
        pk, la = a("PK", 96 * t, 96 * t + 96), a("LA", 96 * t, 96 * t + 96)
        rt, lb = a("RT", 32 * t, 32 * t + 32), a("LB", 32 * t, 32 * t + 32)
        n = len(T.cores); host = (rank + 1 + t % (n - 1)) % n; guest = (rank - 1 - t % (n - 1)) % n
        if t == 0:
            keys("PA", X); cp(a("KI"), a("PA", 0, 32))
        ts(a("KA", 0, 32), a("KI"), 4095, AND)
        ts(a("K16", 0, 32), a("KA", 0, 32), -2048.0, A_)
        cp(a("KA", 32, 64), a("KA", 0, 32)); cp(a("KA", 64, 128), a("KA", 0, 64))
        gid[0] += 2; ga, gb = gid[0] - 1, gid[0]
        ns = 0; sg = []
        for q4, (j0, j1) in enumerate(CHUNKS):
            kb = "KB%d" % (q4 % 2); js = order[j0:j1]; wq = 32 * (j1 - j0)
            it = [(a(kb, 0, wq), ROT(0), a("C2K", 0, wq))]
            for i, j in enumerate(js):
                it.append((a(kb, 32 * i, 32 * i + 32), ROT(j), a("K16", 0, 32)))
                if j:
                    it.append((a(kb, 32 * i, 32 * i + 32), ROT(j - 16), a("K16", 1, 33)))
            mms(it)
            pr = a("PR", 32 * j0, 32 * j1)
            tt(pr, a(kb, 0, wq), a("KA", 0, wq), M); ts(pr, pr, 5, SHR, 4095, AND)
            for i, j in enumerate(js):
                cj = 37 * j + 11 * t; b0 = 32 * (j0 + i); ws = cj // 16 * 16
                ts(a("IX", b0, b0 + 32), a("PR", b0, b0 + 32), float(cj - ws), A_)
                wd = ind(a("D", ws, ws + 4112), a("IX", b0, b0 + 32)); c0 = 513 * j + 1
                if j in SJ:
                    dg, e = a("DG", 512 * (ns % 3), 512 * (ns % 3) + 512), ["E0", "E1", "PB"][ns % 3]; ns += 1
                    act(dg, wd, AF.Identity)
                    if len(sg) > 1:
                        ops[-1]["then"] = sg[-2]
                    mms([(a(e), a("NIB"), a(X, j, j + 512)), (a(e), a("IDB"), dg)])
                    act(a("CMP", c0, c0 + 512), a(e), AF.Sign, bias=-0.5); sg.append(len(ops) - 1)
                else:
                    tt(a("CMP", c0, c0 + 512), wd, a(X, j, j + 512), ALU.is_gt)
                z = Z("ZH" if j in SJ else "Z1", j)
                mm(ga, a("CA", 0, 256), z, a("CMP", c0, c0 + 512, 2))
                mm(gb, a("CB", 0, 256), z, a("CMP", c0 + 1, c0 + 512, 2))
        for k in range(4):
            ts(a("RP", 128 * k, 128 * k + 64), a("CA", k, 256, 4), c(THV), ALU.is_le)
            act(a("RP", 128 * k + 64, 128 * k + 128), a("CB", k, 256, 4), AF.Relu, bias=c(THS), scale=-1.0)
        mms([(a("KB0", 0, 32), Z("Z16", r), a("RP", r, 512, 16)) for r in range(16)])
        act(a("LN1"), a("KB0", 0, 32), AF.Ln, bias=16.0 ** -7)
        ts(a("J1"), a("LN1"), -1.0 / L16, M, 8.415, A_)
        for h in range(4):
            ts(a("OFF", h, 32, 4), a("J1", h, 32, 4), 64.0, M, c(RC + h), A_)
        mms([(a("KB1", 0, 64), Z("Z16", k), a("RP", 64 * k, 64 * k + 64)) for k in range(8)])
        act(a("LN2"), a("KB1", 0, 64), AF.Ln, bias=16.0 ** -8)
        act(a("SG"), a("LN2"), AF.Sign, bias=c(THR), scale=-1.0)
        ts(a("J2"), a("LN2"), -1.0 / L16, M, 8.415, A_)
        ts(a("NS"), a("J2"), 16.0, GE, 528.0, M); tt(a("JJ"), a("J2"), a("NS"), ALU.max)
        act(a("NS1"), a("SG"), AF.Relu)
        tt(a("V0I"), a("KA", 0, 32), a("KA", 0, 32), M); ts(a("V0I"), a("V0I"), 5, SHR, 511, AND); cp(a("V16"), a("V0I"))
        for k in range(16):
            mms([(a("PA", k, 512, 16), a("SEL", 128 * k, 128 * k + 128), a("K16", 0, 32))])
            mms([(a("PB", k, 512, 16), a("SEL", 128 * k, 128 * k + 128), a("V16"))])
        act(a("KR", 0, 512), a("PA"), AF.Identity, bias=2048.0); act(a("PLT", 0, 512), a("PB"), AF.Identity, bias=c(C16))
        for k in range(7, -1, -1):
            ts(a("T1", 64 * k, 64 * k + 32), ind(a("T1", 64 * k + 64, 1536), a("OFF", 4 * k, 4 * k + 2)), a("B128", k, k + 1), A_)
            act(a("T1", 64 * k + 32, 64 * k + 64), ind(a("T1", 64 * k + 64, 1536), a("OFF", 4 * k + 2, 4 * k + 4)), AF.Identity, bias=a("B128", k, k + 1))
        mms([(a("E0", 0, 56), Z("Z8", r), a("T1", 64 * (r // 2) + 8 * (r % 2), 64 * (r // 2) + 8 * (r % 2) + 56)) for r in range(15, -1, -1)])
        for h in range(4):
            ts(a("U2", h, 32, 4), a("E0", 16 * h, 16 * h + 8), c(PC + h), A_)
        for k in range(7, -1, -1):
            tt(a("T2", 64 * k, 64 * k + 64), ind(a("T2", 64 * k + 64, 640), a("U2", 4 * k, 4 * k + 4)), a("CT", 64 * k, 64 * k + 64), A_)
        for s in range(8):
            if s == 0:
                cp(a("CH", 8, 9), a("T2", 0, 1))
            else:
                cp(a("CH", 16 * s, 16 * s + 16), ind(a("T2"), a("CH", 16 * s - 8, 16 * s - 7)))
            wu = ind(a("T1"), a("CH", 16 * s + 8, 16 * s + 9))
            if s < 7:
                act(a("UR", 8 * s, 8 * s + 16), wu, AF.Relu, bias=-100.0)
            else:
                ts(a("UU", 0, 56), a("UR", 0, 56), 1.0, ALU.min)
                ts(a("UU", 56, 72), wu, 100.0, GE)
        uu = a("UU", 0, 64)
        tt(a("W1", 2, 66), uu, a("SG"), M); tt(a("AW"), uu, a("NS1"), M); tt(a("W2"), uu, a("JJ"), M)
        mms([(a("E1", 0, 32), a("TP", 512 + 128 * p, 640 + 128 * p), a("UU", p, 64, 2)) for p in range(2)] +
            [(a("E1", 0, 32), a("TP", 128 * s, 128 * s + 128), a("W1", s, s + 63, 2)) for s in range(4)])
        mms([(a("KB1", 0, 32), ROT(0), a("VC"))] + [(a("KB1", 0, 32), a("BP", 128 * p, 128 * p + 128), a("AW", p, 64, 2)) for p in range(2)])
        mms([(a("KB0", 0, 32), ROT(0), a("Q16")), (a("KB0", 0, 32), ROT(0), a("W2", 0, 64, 2)), (a("KB0", 0, 32), ROT(-8), a("W2", 1, 64, 2))])
        diag(a("KB1", 0, 32), "VD", "VL"); vu = a("VU", 2 * t, 2 * t + 2); cp(vu, a("VL", 0, 2))
        cp(pk0, ind(a(X, 0, 1040), vu)); act(pk1, ind(a("KR"), vu), AF.Identity); cp(pk2, ind(a("PLT"), vu))
        sa = send(pk, la, "a%d" % t, host)
        if t < RO - 1:
            mms([(a("E0", 0, 32), ROT(0), a("AW", 0, 64, 2)), (a("E0", 0, 32), ROT(-8), a("AW", 1, 64, 2))])
            act(a("AWN"), a("E0", 0, 32), AF.Identity)
        act(a("RL"), a("E1", 0, 32), AF.Relu, scale=c(NN4))
        act(a("LN3"), a("RL"), AF.Ln, bias=4.0 ** -18)
        ts(a("J3"), a("LN3"), -1.0 / L4, M, -0.04, A_)
        tt(a("LF"), a("J3"), a("QB"), A_); ts(a("LU"), a("LF"), 512.0, M)
        ts(a("MV"), a("RL"), 0.0, ALU.is_gt); tt(a("SRI"), a("KB0", 0, 32), a("MV"), SUB); cp(a("SRU"), a("SRI"))
        for h in range(2):
            act(a("INC", 256 * h, 256 * h + 256), ind(a("CMP"), a("LU", 16 * h, 16 * h + 16)), AF.Relu)
            tt(a(XN, 256 * h, 256 * h + 256), ind(a(X, 0, 1040), a("SRU", 16 * h, 16 * h + 16)), a("INC", 256 * h, 256 * h + 256), A_)
        act(a(XN, 512, 528), a(XN, 0, 16), AF.Identity)
        ts(a("SOT"), a("SRI"), 528.0, GE, -528.0, M); tt(a("SOI"), a("SRI"), a("SOT"), A_); cp(a("SOU"), a("SOI"))
        act(a(ON, 0, 512), ind(a(O, 0, 512), a("SOU")), AF.Identity)
        recv(la, "a%d" % t, guest, sa)
        cp(a("PLU"), la2)
        cp(a("PLI"), la2); ts(a("PLI"), a("PLI"), 511, AND); tt(a("PLD"), a("F1"), a("PLI"), SUB)
        act(a("VXH"), la0, AF.Identity); act(a(XN, 1040, 1072), la0, AF.Identity)
        act(a("INV"), la0, AF.Relu, scale=-1.0)
        cp(a("XG", 0, 256), ind(a(XN, 0, 528), a("PLU", 0, 16)))
        act(a("XG", 256, 512), ind(a(XN, 0, 528), a("PLU", 16, 32)), AF.Identity)
        keys("PA", "XG")
        cp(a("K2"), a("PA", 0, 32)); ts(a("K2"), a("K2"), 4095, AND); tt(a("K2"), a("K2"), la1, M)
        ts(a("K2"), a("K2"), 5, SHR, 4095, AND); ts(a("IX2"), a("K2"), c(CJ + t), A_)
        tt(a("CM2"), ind(a("D"), a("IX2")), a("XG"), ALU.is_gt)
        mms([(a("PB", 0, 32), a("IDB"), a("INV"))] + [(a("PB", 0, 32), Z("Z1", r), a("CM2", r, 512, 16)) for r in range(16)])
        ts(a("EP"), a("PB", 0, 32), 8.0, ALU.is_le)
        mms([(a("CA", 0, 32), a("IDB"), a("PLD")), (a("CA", 0, 32), a("TRI"), a("EP"))])
        ts(a("FP"), a("CA", 0, 32), 0.0, ALU.max)
        mms([(a("CB", 0, 96), ROT(0), a("CC3"))] + [(a("CB", 32 * k, 32 * k + 32), a("NBL"), a("FP")) for k in range(3)])
        diag(a("CB", 0, 32), "CD", "CL")
        for h in range(2):
            ts(a("EQ", 32 * h, 32 * h + 32), a("CB", 32 + 32 * h, 64 + 32 * h), a("CL", h, h + 1), ALU.is_equal)
            red(a("LO", h, h + 1), a("EQ", 32 * h, 32 * h + 32), ALU.max)
            ts(a("FI", h, h + 1), a("LO", h, h + 1), c(DUMC + h), M, a("CL", h, h + 1), ALU.max)
        fi = ind(a(XN), a("FI", 0, 2))
        cp(rt, fi)
        sb = send(rt, lb, "b%d" % t, guest)
        cp(fi, a("VXH"))
        recv(lb, "b%d" % t, host, sb)
        if t < RO - 1:
            ms(a(XN, 512, 528), -64.0)
            keys("PA", XN); act(a("KP"), a("PA", 0, 32), AF.Identity)
            mms([(a("PB", 0, 32), a("BW"), a("C64")), (a("PB", 0, 32), a("BW"), lb)])
            tt(a("KT"), a("PB", 0, 32), a("AWN"), M); tt(a("KI"), a("KT"), a("KP"), A_)
            cp(ind(a(XN, 0, 1040), vu), lb)
        else:
            dma("Y", lambda q: q.dma_start(T.yseat[:], T[ON][0:128:16, 0:512]), [], [a(ON, 0, 512)], "dz", 2000)
            mms([(a("E0", 0, 32), Z("Z8F", r), a(ON, r, 512, 16)) for r in range(16)], 4)
            cp(a("OLU"), a("E0", 0, 32))
            act(a("VP"), ind(a(ON), vu), AF.Identity)
            diag(a("VP"), "VD", "VQ"); cp(a("VPU", 0, 2), a("VQ", 0, 2))
            cp(ind(a("Y", 0, 512), a("OLU")), a(XN, 0, 512))
            cp(ind(a("Y"), a("VPU", 0, 2)), lb)
            dma("Y", lambda q: q.dma_start(T.ypup[:], T.Y[:, 0:512]), [], [a("Y", 0, 512)], "dy", 2000)
    return ops


def meet(x, y):
    if x[1] >= y[2] or y[1] >= x[2]:
        return False
    return not (x[3] == y[3] and x[3] > 1 and (x[1] - y[1]) % x[3])


def plan(ops):
    seen = {}; first = {}
    for i, o in enumerate(ops):
        dep = set()
        for sp, w in [(s, False) for s in o["rd"]] + [(s, True) for s in o["wr"]]:
            for j, s2, w2 in seen.get(sp[0], []):
                p = ops[j]
                if sp[0] in PS:
                    if "grp" in o and p.get("grp") == o["grp"]:
                        continue
                    if p["eng"] != o["eng"] or o["eng"] == "P":
                        dep.add(j)
                elif (w or w2) and meet(sp, s2):
                    dep.add(j)
        for sp, w in [(s, False) for s in o["rd"]] + [(s, True) for s in o["wr"]]:
            seen.setdefault(sp[0], []).append((i, sp, w))
        if o.get("lead"):
            if o["grp"] in first:
                dep.add(first[o["grp"]])
            else:
                first[o["grp"]] = i
        if o["eng"] == "R":
            assert not dep
        dep.discard(i)
        o["dep"] = dep; o["sdep"] = dep | {o[k] for k in ("after", "then") if k in o}
    n = len(ops); succ = [[] for _ in ops]; left = [len(o["sdep"]) for o in ops]
    for i, o in enumerate(ops):
        for j in o["sdep"]:
            succ[j].append(i)
    pred = [sorted(o["sdep"]) for o in ops]
    en = [o["eng"] for o in ops]; co = [o["cost"] for o in ops]; la = [o.get("lat", 0) for o in ops]

    def sched(prio, nxt, prv, back, look):
        left = [len(p) for p in prv]; free = {}; fin = [0.0] * n; seq = []
        rdy = [la[i] if back else 0.0 for i in range(n)]; ready = {}
        for i in range(n):
            if not left[i]:
                ready.setdefault(en[i], []).append(i)
        while len(seq) < n:
            t0, eng = min((max(min(rdy[i] for i in r), free.get(e, 0.0)), e) for e, r in ready.items() if r)
            r = ready[eng]
            e0 = max((i for i in r if rdy[i] <= t0), key=lambda i: (prio[i], -i))
            best = max((i for i in r if rdy[i] <= t0 + look * co[e0] + 20), key=lambda i: (prio[i], -i))
            r.remove(best); seq.append(best)
            free[eng] = fin[best] = max(rdy[best], t0) + co[best]
            for j in nxt[best]:
                d = la[j if back else best] + (0 if eng == "P" and en[j] == "P" else LAT)
                if ops[best if back else j].get("then", -1) == (j if back else best):
                    d = 0
                rdy[j] = max(rdy[j], fin[best] + d); left[j] -= 1
                if not left[j]:
                    ready.setdefault(en[j], []).append(j)
        return seq, fin, max(fin[i] + (0 if back else la[i]) for i in range(n))

    prio = [0.0] * n
    for i in range(n - 1, -1, -1):
        prio[i] = co[i] + la[i] + max([prio[j] + LAT for j in succ[i]] + [0.0])
    top = None
    for look in LOOKS:
        p = prio
        for it in range(PASSES):
            seq, fin, span = sched([p[i] + ops[i]["up"] for i in range(n)], succ, pred, False, look)
            if top is None or span < top[2]:
                top = (seq, fin, span)
            p = sched(fin, pred, succ, True, look)[1]
    seq = top[0]
    first = {}
    pos = {}; cnt = {}
    for i in seq:
        e = ops[i]["eng"]; cnt[e] = cnt.get(e, 0) + 1; pos[i] = cnt[e]; ops[i]["t"] = top[1][i] - co[i]
        if "grp" in ops[i]:
            first.setdefault(ops[i]["grp"], i)
    know = {}; need = set(); last = {}
    for i in seq:
        o = ops[i]; e = o["eng"]; k = know.setdefault(e, {}); o["waits"] = []
        want = {}
        for j in o["dep"]:
            p = ops[j]
            if "dsem" in p:
                want[p["dsem"]] = (1, j)
            elif not (e == "P" and p["eng"] == "P") and want.get(p["eng"], (0, 0))[0] < pos[j]:
                want[p["eng"]] = (pos[j], j)
        for key, (v, j) in sorted(want.items(), key=lambda kv: -ops[kv[1][1]]["t"]):
            if k.get(key, 0) < v:
                o["waits"].append(j); need.add(j); k[key] = v
                for kk, vv in ops[j]["know"].items():
                    if k.get(kk, 0) < vv:
                        k[kk] = vv
        o["know"] = dict(k)
        if "grp" in o:
            last[o["grp"]] = i
    return seq, need, first, last


PLAN = []


def rank_program(g, core, T, topo):
    rank = T.rank_of(core)
    if rank is None:
        return
    ops = build(T, topo, core, rank)
    if not PLAN:
        PLAN.append((ops, plan(ops)))
    po, (seq, need, first, last) = PLAN[0]
    Q = {"V": g.vector, "S": g.scalar, "P": g.tensor, "G": g, "Y": g.sync}
    val = {}; cnt = {}; sent = 0
    for i in seq:
        o = ops[i]; e = o["eng"]
        if "dsem" in o:
            val[i] = (o["dsem"], o["dn"])
        elif i in need:
            cnt[e] = cnt.get(e, 0) + 1; val[i] = (ESEM[e], cnt[e])
        if e == "R":
            continue
        q = Q[e]
        for j in po[i]["waits"]:
            q.wait_ge(T.sem[val[j][0]], val[j][1])
        r = o["fn"](q, first[o["grp"]] == i, last[o["grp"]] == i) if "grp" in o else o["fn"](q)
        if "remote" in o:
            sent += o["remote"]
        elif i in val:
            r.then_inc(T.sem[val[i][0]], 16 if "dsem" in o else 1)
    g.wait_ge(T.sem["sent"], sent)
    g.sync.wait_ge(T.sem["dz"], 16); g.sync.wait_ge(T.sem["dy"], 16)
